import numpy as np
import ml_dtypes

BF16 = ml_dtypes.bfloat16


def bf(x):
    return np.asarray(x, np.float32).astype(BF16)


def f32(x):
    return np.asarray(x, np.float32)


def f64(x):
    return np.asarray(x).astype(np.float64)


def striped(idx):
    return np.concatenate([l.reshape(-1, 16).T for l in idx])


def rows(idx, k):
    return np.tile(np.repeat(idx, 16, axis=0), (k // (16 * 8), 1))


def look(tab, idx):
    return np.take_along_axis(f64(tab), rows(idx, len(tab)), axis=1)


K, S, V, N, M = 128, 2048, 1536, 1536, 256


def setup_inputs():
    return {"tab": f32(np.random.standard_normal((2, K, S))), "y": f32(np.random.standard_normal((K, V))), "w": bf(np.random.standard_normal((K, M)) / np.sqrt(K)), "b": f32(0.5 * np.random.standard_normal((M, 1))), "offs": striped(np.stack([np.random.permutation(S)[:N] for _ in range(8)]))}


def reference(tab, y, w, b, offs):
    idx = np.stack([g.T.reshape(-1) for g in np.split(offs, 8)])
    x = (look(tab[0], idx) - f64(y)) * (np.tanh(look(tab[1], idx)))
    return np.maximum(f64(w).T @ x + f64(b), 0.0)

@@ -1,0 +1,69 @@
+import concourse.mybir as mybir
+
+P = 128
+PLACES = 2048
+N = 1536
+M = 256
+PIECE = 512
+PIECES = N // PIECE
+OFFSET_COLUMNS = PIECE // 16
+
+F32, BF16, U16 = mybir.dt.float32, mybir.dt.bfloat16, mybir.dt.uint16
+ADD, SUBTRACT = mybir.AluOpType.add, mybir.AluOpType.subtract
+MULT, MAX = mybir.AluOpType.mult, mybir.AluOpType.max
+TANH, RELU = mybir.ActivationFunctionType.Tanh, mybir.ActivationFunctionType.Relu
+
+FLOPS = 2 * P * M * N
+
+
+def tile_lookup_vg_subtanh_relu_kernel(tc, tab, y, w, b, offs, out):
+    nc = tc.nc
+    with (
+        tc.tile_pool(name="held", bufs=1) as held,
+        tc.tile_pool(name="work", bufs=PIECES) as work,
+        tc.psum_pool(name="psum", bufs=PIECES) as psum,
+    ):
+        offsets = held.tile([P, N // 16], U16, name="offsets")
+        nc.sync.dma_start(offsets[:], offs)
+        values = held.tile([P, PLACES], F32, name="values")
+        nc.sync.dma_start(values[:], tab[0])
+        stream = held.tile([P, N], F32, name="stream")
+        nc.sync.dma_start(stream[:], y)
+        gates = held.tile([P, PLACES], F32, name="gates")
+        nc.sync.dma_start(gates[:], tab[1])
+        weights = held.tile([P, M], BF16, name="weights")
+        nc.sync.dma_start(weights[:], w)
+        bias = held.tile([P, M // P], F32, name="bias")
+        nc.sync.dma_start(bias[:], b.rearrange("(t p) o -> p (t o)", p=P))
+
+        differences, gated = [], []
+        for i in range(PIECES):
+            entries = offsets[:, i * OFFSET_COLUMNS : (i + 1) * OFFSET_COLUMNS]
+            difference = work.tile([P, PIECE], F32, name="difference")
+            nc.vector.tensor_tensor(
+                difference[:], values[:].indirect(entries),
+                stream[:, i * PIECE : (i + 1) * PIECE], SUBTRACT,
+            )
+            differences.append(difference)
+            gate = work.tile([P, PIECE], F32, name="gate")
+            nc.scalar.activation(gate[:], gates[:].indirect(entries), TANH)
+            gated.append(gate)
+
+        for i in range(PIECES):
+            x = work.tile([P, PIECE], BF16, name="x")
+            nc.vector.tensor_tensor(x[:], differences[i][:], gated[i][:], MULT)
+            for t in range(M // P):
+                layer = psum.tile([P, PIECE], F32, name=f"layer{t}")
+                nc.tensor.matmul(
+                    layer[:], weights[:, t * P : (t + 1) * P], x[:], start=True, stop=True
+                )
+                result = work.tile([P, PIECE], F32, name=f"result{t}")
+                if t == 0:
+                    nc.scalar.activation(result[:], layer[:], RELU, bias=bias[:, t : t + 1])
+                else:
+                    nc.vector.tensor_scalar(
+                        result[:], layer[:], bias[:, t : t + 1], 0.0, op0=ADD, op1=MAX
+                    )
+                nc.sync.dma_start(
+                    out[t * P : (t + 1) * P, i * PIECE : (i + 1) * PIECE], result[:]
+                )

@@ -23,14 +23,21 @@ def tile_lookup_vg_subtanh_relu_kernel(tc, tab, y, w, b, offs, out):
         tc.tile_pool(name="work", bufs=PIECES) as work,
         tc.psum_pool(name="psum", bufs=PIECES) as psum,
     ):
+        zeros = held.tile([P, 1], F32, name="zeros")
+        nc.vector.memset(zeros[:], 0.0)
+        warm = held.tile([P, 1], F32, name="warm")
+        nc.scalar.activation(warm[:], zeros[:], TANH)
+
         offsets = held.tile([P, N // 16], U16, name="offsets")
         nc.sync.dma_start(offsets[:], offs)
         values = held.tile([P, PLACES], F32, name="values")
         nc.sync.dma_start(values[:], tab[0])
-        stream = held.tile([P, N], F32, name="stream")
-        nc.sync.dma_start(stream[:], y)
+        stream = [held.tile([P, PIECE], F32, name=f"stream{i}") for i in range(PIECES)]
         gates = held.tile([P, PLACES], F32, name="gates")
-        nc.sync.dma_start(gates[:], tab[1])
+        for i in range(PIECES):
+            nc.sync.dma_start(stream[i][:], y[:, i * PIECE : (i + 1) * PIECE])
+            if i == 0:
+                nc.sync.dma_start(gates[:], tab[1])
         weights = held.tile([P, M], BF16, name="weights")
         nc.sync.dma_start(weights[:], w)
         bias = held.tile([P, M // P], F32, name="bias")
@@ -42,13 +49,14 @@ def tile_lookup_vg_subtanh_relu_kernel(tc, tab, y, w, b, offs, out):
             difference = work.tile([P, PIECE], F32, name="difference")
             nc.vector.tensor_tensor(
                 difference[:], values[:].indirect(entries),
-                stream[:, i * PIECE : (i + 1) * PIECE], SUBTRACT,
+                stream[i][:], SUBTRACT,
             )
             differences.append(difference)
             gate = work.tile([P, PIECE], F32, name="gate")
             nc.scalar.activation(gate[:], gates[:].indirect(entries), TANH)
             gated.append(gate)
 
+        layers = []
         for i in range(PIECES):
             x = work.tile([P, PIECE], BF16, name="x")
             nc.vector.tensor_tensor(x[:], differences[i][:], gated[i][:], MULT)
@@ -57,13 +65,14 @@ def tile_lookup_vg_subtanh_relu_kernel(tc, tab, y, w, b, offs, out):
                 nc.tensor.matmul(
                     layer[:], weights[:, t * P : (t + 1) * P], x[:], start=True, stop=True
                 )
-                result = work.tile([P, PIECE], F32, name=f"result{t}")
-                if t == 0:
-                    nc.scalar.activation(result[:], layer[:], RELU, bias=bias[:, t : t + 1])
-                else:
-                    nc.vector.tensor_scalar(
-                        result[:], layer[:], bias[:, t : t + 1], 0.0, op0=ADD, op1=MAX
-                    )
-                nc.sync.dma_start(
-                    out[t * P : (t + 1) * P, i * PIECE : (i + 1) * PIECE], result[:]
+                layers.append((i, t, layer))
+
+        for i, t, layer in layers:
+            result = work.tile([P, PIECE], F32, name=f"result{t}")
+            if i == 0 or t == 0:
+                nc.scalar.activation(result[:], layer[:], RELU, bias=bias[:, t : t + 1])
+            else:
+                nc.vector.tensor_scalar(
+                    result[:], layer[:], bias[:, t : t + 1], 0.0, op0=ADD, op1=MAX
                 )
+            nc.sync.dma_start(out[t * P : (t + 1) * P, i * PIECE : (i + 1) * PIECE], result[:])

import concourse.mybir as mybir

P = 128
PLACES = 2048
N = 1536
M = 256
PIECE = 512
PIECES = N // PIECE
OFFSET_COLUMNS = PIECE // 16

F32, BF16, U16 = mybir.dt.float32, mybir.dt.bfloat16, mybir.dt.uint16
ADD, SUBTRACT = mybir.AluOpType.add, mybir.AluOpType.subtract
MULT, MAX = mybir.AluOpType.mult, mybir.AluOpType.max
TANH, RELU = mybir.ActivationFunctionType.Tanh, mybir.ActivationFunctionType.Relu

FLOPS = 2 * P * M * N


def tile_lookup_vg_subtanh_relu_kernel(tc, tab, y, w, b, offs, out):
    nc = tc.nc
    with (
        tc.tile_pool(name="held", bufs=1) as held,
        tc.tile_pool(name="work", bufs=PIECES) as work,
        tc.psum_pool(name="psum", bufs=PIECES) as psum,
    ):
        zeros = held.tile([P, 1], F32, name="zeros")
        nc.vector.memset(zeros[:], 0.0)
        warm = held.tile([P, 1], F32, name="warm")
        nc.scalar.activation(warm[:], zeros[:], TANH)

        offsets = held.tile([P, N // 16], U16, name="offsets")
        nc.sync.dma_start(offsets[:], offs)
        values = held.tile([P, PLACES], F32, name="values")
        nc.sync.dma_start(values[:], tab[0])
        stream = [held.tile([P, PIECE], F32, name=f"stream{i}") for i in range(PIECES)]
        gates = held.tile([P, PLACES], F32, name="gates")
        for i in range(PIECES):
            nc.sync.dma_start(stream[i][:], y[:, i * PIECE : (i + 1) * PIECE])
            if i == 0:
                nc.sync.dma_start(gates[:], tab[1])
        weights = held.tile([P, M], BF16, name="weights")
        nc.sync.dma_start(weights[:], w)
        bias = held.tile([P, M // P], F32, name="bias")
        nc.sync.dma_start(bias[:], b.rearrange("(t p) o -> p (t o)", p=P))

        differences, gated = [], []
        for i in range(PIECES):
            entries = offsets[:, i * OFFSET_COLUMNS : (i + 1) * OFFSET_COLUMNS]
            difference = work.tile([P, PIECE], F32, name="difference")
            nc.vector.tensor_tensor(
                difference[:], values[:].indirect(entries),
                stream[i][:], SUBTRACT,
            )
            differences.append(difference)
            gate = work.tile([P, PIECE], F32, name="gate")
            nc.scalar.activation(gate[:], gates[:].indirect(entries), TANH)
            gated.append(gate)

        layers = []
        for i in range(PIECES):
            x = work.tile([P, PIECE], BF16, name="x")
            nc.vector.tensor_tensor(x[:], differences[i][:], gated[i][:], MULT)
            for t in range(M // P):
                layer = psum.tile([P, PIECE], F32, name=f"layer{t}")
                nc.tensor.matmul(
                    layer[:], weights[:, t * P : (t + 1) * P], x[:], start=True, stop=True
                )
                layers.append((i, t, layer))

        for i, t, layer in layers:
            result = work.tile([P, PIECE], F32, name=f"result{t}")
            if i == 0 or t == 0:
                nc.scalar.activation(result[:], layer[:], RELU, bias=bias[:, t : t + 1])
            else:
                nc.vector.tensor_scalar(
                    result[:], layer[:], bias[:, t : t + 1], 0.0, op0=ADD, op1=MAX
                )
            nc.sync.dma_start(out[t * P : (t + 1) * P, i * PIECE : (i + 1) * PIECE], result[:])
